import numpy as np
import ml_dtypes


def mxq(x, axis, fmt="e4m3"):
    dtype, down = {"e4m3": (ml_dtypes.float8_e4m3fn, 7), "e5m2": (ml_dtypes.float8_e5m2, 14)}[fmt]
    v = np.moveaxis(np.asarray(x, np.float32).astype(ml_dtypes.bfloat16).astype(np.float64), axis, -1)
    blocks = v.reshape(v.shape[:-1] + (-1, 32))
    amax = np.abs(blocks).max(-1, keepdims=True)
    byte = np.maximum(np.where(amax > 0, np.frexp(amax)[1] - 1 + 127, 0) - down, 1)
    scale = np.exp2(byte - 127.0)
    codes = (blocks / scale).astype(np.float32).astype(dtype).astype(np.float64)
    return np.moveaxis((codes * scale).reshape(v.shape), -1, axis)


WIDE = False


def mx_kscale(k):
    if not WIDE:
        return np.ones(k)
    levels = np.array([10, -10, 5, -5, 0])
    if k % 512:
        return np.exp2(np.random.permutation(np.resize(levels, k // 32))).repeat(32)
    a = np.empty((k // 512, 16))
    for p in range(k // 512):
        a[p, :8] = np.random.permutation(np.resize(levels, 8))
        for g in range(8):
            far = levels[np.abs(levels - a[p, g]) >= 10]
            a[p, g + 8] = far[np.random.randint(len(far))]
    return np.exp2(a.ravel()).repeat(32)


def f64(x):
    return np.asarray(x).astype(np.float64)


def striped(idx):
    return np.tile(idx.reshape(-1, 16).T, (8, 1)).astype(np.uint16)


def unstriped(offs):
    return offs[:16].T.reshape(-1).astype(np.int64)


E2M1 = np.array([0.0, 0.5, 1.0, 1.5, 2.0, 3.0, 4.0, 6.0, -0.0, -0.5, -1.0, -1.5, -2.0, -3.0, -4.0, -6.0])


def pack_weight(w, fmt):
    k, n = w.shape
    w = f64(np.asarray(w, np.float32).astype(ml_dtypes.bfloat16)).reshape(k // 32, 32, n)
    amax = np.abs(w).max(1)
    if fmt == "e4m3":
        byte = np.frexp(amax)[1] - 1 + 127 - 7
    else:
        mant, ex = np.frexp(amax / 6.0)
        byte = np.where(mant > 0.5, ex, ex - 1) + 127
    byte = np.clip(np.where(amax > 0, byte, 1), 1, 254)
    scaled = (w * np.exp2(127.0 - byte)[:, None, :]).reshape(k, n).astype(np.float32)
    by_word = np.ascontiguousarray(scaled.reshape(k // 512, 128, 4, n).transpose(0, 1, 3, 2))
    if fmt == "e4m3":
        words = by_word.astype(ml_dtypes.float8_e4m3fn).view(np.uint8)
    else:
        c = by_word.astype(ml_dtypes.float4_e2m1fn).view(np.uint8) & 0xF
        words = (c[..., 0::2] | (c[..., 1::2] << 4)).reshape(k // 512, 128, 2 * n)
    return np.ascontiguousarray(words), np.ascontiguousarray(byte.astype(np.uint8).reshape(k // 512, 16, n))


def unpack_weight(words, scales, fmt):
    g, _, n = scales.shape
    words = np.ascontiguousarray(words).reshape(g, 128, n, -1)
    if fmt == "e4m3":
        vals = words.view(ml_dtypes.float8_e4m3fn).astype(np.float64)
    else:
        nib = np.empty((g, 128, n, 4), np.uint8)
        nib[..., 0::2] = words & 0xF
        nib[..., 1::2] = words >> 4
        vals = E2M1[nib]
    vals = vals * np.repeat(np.exp2(scales.astype(np.float64) - 127.0), 8, axis=1)[..., None]
    return vals.transpose(0, 1, 3, 2).reshape(g * 512, n)


def gelu(v):
    return 0.5 * v * (1.0 + np.tanh(np.sqrt(2.0 / np.pi) * (v + 0.044715 * v**3)))


K, T, S, S2 = 1024, 2048, 512, 1024


def setup_inputs():
    n = np.random.standard_normal
    s = mx_kscale(K)[:, None]
    d = {}
    d["tab_words"], d["tab_scales"] = pack_weight(n((K, T)) * s, "e4m3")
    d["offs"] = striped(np.random.permutation(T)[:S])
    d["offs2"] = striped(np.random.permutation(T)[:S2])
    d["w1_words"], d["w1_scales"] = pack_weight(1.4 * n((K, K)) / (K * s * s.T), "e2m1")
    d["w2"] = (n((K, K)) / (K ** 0.5 * s)).astype(np.float32)
    d["gain"] = (np.exp(0.4 * n(K)) / (K ** 0.5 * s[:, 0])).astype(np.float32)
    d["w3"] = (n((K, S2)) / (K ** 0.5 * s)).astype(np.float32)
    return d


def reference(tab_words, tab_scales, offs, offs2, w1_words, w1_scales, w2, gain, w3):
    TW = unpack_weight(tab_words, tab_scales, "e4m3")
    v = TW[:, unstriped(offs)]
    v2 = TW[:, unstriped(offs2)]
    w1 = unpack_weight(w1_words, w1_scales, "e2m1")
    h1 = np.maximum(w1.T @ v, 0.0)
    e1 = v2.T @ mxq(h1, 0, "e4m3")
    h2 = f64(gain)[:, None] * (mxq(f64(w2), 0, "e4m3").T @ v)
    e2 = v2.T @ mxq(h2, 0, "e4m3")
    e3 = mxq(f64(w3), 0, "e4m3").T @ v
    return np.maximum(e1, e2) / (1.0 + np.abs(e3))

@@ -1,0 +1,244 @@
+from contextlib import ExitStack
+
+import concourse.mybir as mybir
+
+K, T, S, S2 = 1024, 2048, 512, 1024
+FLOPS = 5 * 2 * K * K * S
+
+F32 = mybir.dt.float32
+BF16 = mybir.dt.bfloat16
+I32 = mybir.dt.int32
+U32 = mybir.dt.uint32
+U16 = mybir.dt.uint16
+U8 = mybir.dt.uint8
+FP8X4 = mybir.dt.float8_e4m3fn_x4
+FP4X4 = mybir.dt.float4_e2m1fn_x4
+ACT = mybir.ActivationFunctionType
+ALU = mybir.AluOpType
+
+P = 128
+PASSES = 2
+HALF = 256
+
+
+def tile_list_bout_contest_scores_kernel(
+    tc, tab_words, tab_scales, offs, offs2, w1_words, w1_scales, w2, gain, w3, out
+):
+    nc = tc.nc
+    with ExitStack() as ctx:
+        keep = ctx.enter_context(tc.tile_pool(name="keep", bufs=1))
+        ring = ctx.enter_context(tc.tile_pool(name="ring", bufs=3))
+        psum = ctx.enter_context(tc.psum_pool(name="psum", bufs=4))
+
+        def held(shape, dtype, name):
+            return keep.tile(shape, dtype, name=name, align_bytes=64)
+
+        east = keep.tile([P, S // 16], U16, name="east")
+        west = keep.tile([P, S2 // 16], U16, name="west")
+        tab_sc = held([P, T], U8, "tab_sc")
+        w1_sc_raw = held([P, PASSES * K], U8, "w1_sc_raw")
+        tab_sc_high = held([P, T], U8, "tab_sc_high")
+        nc.vector.memset(tab_sc[:].bitcast(I32), 0)
+        nc.vector.memset(w1_sc_raw[:].bitcast(I32), 0)
+        warm = held([P, 16], F32, "warm")
+        nc.gpsimd.memset(warm[:, 0:8], 1.0)
+        nc.scalar.activation(warm[:, 8:9], warm[:, 0:1], ACT.Abs_reciprocal_sqrt, bias=1.0)
+        nc.vector.memset(tab_sc_high[:].bitcast(I32), 0)
+
+        w1_raw = held([P, PASSES * 2 * K], U8, "w1_raw")
+        tab = [held([P, T], I32, "tab%d" % a) for a in range(PASSES)]
+        gain_sb = held([P, 8], F32, "gain_sb")
+
+        def load_rows(w, a, c0, width, name):
+            raw = held([P, 4, width], F32, name)
+            rows = w[512 * a : 512 * (a + 1), c0 : c0 + width]
+            nc.sync.dma_start(raw[:], rows.rearrange("(p i) c -> p i c", i=4))
+            return raw
+
+        tab_hbm = [tab_words[a].rearrange("p t i -> p (t i)").bitcast(I32) for a in range(PASSES)]
+        w2_raw = {}
+        nc.sync.dma_start(east[:], offs)
+        nc.sync.dma_start(
+            w1_raw[:].bitcast(I32).rearrange("p (a c) -> p a c", a=PASSES),
+            w1_words.bitcast(I32).rearrange("a p c -> p a c"),
+        )
+        for q in range(4):
+            nc.sync.dma_start(
+                tab_sc[32 * q : 32 * q + 8, :].bitcast(I32),
+                tab_scales[:, 4 * q : 4 * q + 4, :].bitcast(I32),
+            )
+        nc.sync.dma_start(tab[0][:], tab_hbm[0])
+        for q in range(4):
+            nc.sync.dma_start(
+                w1_sc_raw[32 * q : 32 * q + 4, :].bitcast(I32).rearrange("r (a c) -> r a c", a=PASSES),
+                w1_scales[:, 4 * q : 4 * q + 4, :].bitcast(I32).rearrange("a r c -> r a c"),
+            )
+        nc.sync.dma_start(tab[1][:], tab_hbm[1])
+        for q in range(4):
+            nc.sync.dma_start(
+                tab_sc_high[32 * q : 32 * q + 4, :].bitcast(I32),
+                tab_scales[1, 4 * q : 4 * q + 4, :].bitcast(I32),
+            )
+        w2_raw[0, 0, 0] = load_rows(w2, 0, 0, HALF, "w2_first0")[:]
+        nc.sync.dma_start(west[:], offs2)
+        nc.sync.dma_start(
+            gain_sb[:].rearrange("p (b t) -> p b t", t=4),
+            gain.rearrange("(b p t) -> p b t", p=P, t=4),
+        )
+        w2_raw[0, 0, 1] = load_rows(w2, 0, HALF, HALF, "w2_first1")[:]
+        for b in range(2):
+            for a in range(PASSES):
+                if (a, b) != (0, 0):
+                    raw = load_rows(w2, a, 512 * b, 512, "w2_raw%d%d" % (a, b))
+                    for h in range(2):
+                        w2_raw[a, b, h] = raw[:, :, HALF * h : HALF * (h + 1)]
+        w3_raw = {}
+        for b in range(2):
+            for a in range(PASSES):
+                raw = load_rows(w3, a, 512 * b, 512, "w3_raw%d%d" % (a, b))
+                for h in range(2):
+                    w3_raw[a, 2 * b + h] = raw[:, :, HALF * h : HALF * (h + 1)]
+
+        w1_cd = held([P, PASSES * 2 * K], U8, "w1_cd")
+        w1_sc = held([P, PASSES * K], U8, "w1_sc")
+        nc.vector.tensor_copy(
+            w1_cd[:].bitcast(U16).rearrange("p (g t u q) -> p g u t q", g=4, t=4, q=8),
+            w1_raw[:].bitcast(U16).rearrange("p (g u q t) -> p g u t q", g=4, t=4, q=8),
+        )
+        v_sc = held([P, S], U8, "v_sc")
+        v_sc_high = held([P, S], U8, "v_sc_high")
+        v_cd = [held([P, S], U32, "v_cd%d" % a) for a in range(PASSES)]
+        v2_cd = [held([P, S2], U32, "v2_cd%d" % a) for a in range(PASSES)]
+        v2_sc = held([P, S2], U8, "v2_sc")
+        nc.vector.tensor_copy(v_cd[0][:], tab[0][:].bitcast(U32).indirect(east[:]))
+        nc.vector.tensor_copy(v_sc[:], tab_sc[:].indirect(east[:]))
+        nc.vector.tensor_copy(
+            w1_sc[:].rearrange("p (g t u q) -> p g u t q", g=4, t=4, q=16),
+            w1_sc_raw[:].rearrange("p (g u q t) -> p g u t q", g=4, t=4, q=16),
+        )
+        nc.vector.tensor_copy(v_cd[1][:], tab[1][:].bitcast(U32).indirect(east[:]))
+        nc.vector.tensor_copy(v_sc_high[:], tab_sc_high[:].indirect(east[:]))
+        nc.vector.tensor_copy(v2_sc[:], tab_sc[:].indirect(west[:]))
+        for a in range(PASSES):
+            nc.vector.tensor_copy(v2_cd[a][:], tab[a][:].bitcast(U32).indirect(west[:]))
+
+        def quantise(grouped, width, name):
+            codes = held([P, width], U32, name + "_cd")
+            scales = held([P, width], U8, name + "_sc")
+            nc.vector.quantize_mx(out=codes[:].bitcast(FP8X4), scales=scales[:], in_=grouped[:])
+            return codes, scales
+
+        def first_stage_bank(tag, lhs, b, jq, v_scales):
+            bank = psum.tile([P, 4 * P], F32, name=tag)
+            cols = slice(P * jq, P * (jq + 1))
+            for t in range(4):
+                for a in range(PASSES):
+                    codes, scales = lhs(a, b, t)
+                    nc.tensor.matmul_mx(
+                        out=bank[:, P * t : P * (t + 1)],
+                        lhsT=codes,
+                        lhsT_scale=scales,
+                        rhs=v_cd[a][:, cols].bitcast(FP8X4),
+                        rhs_scale=v_scales[a][:, cols],
+                        start=(a == 0),
+                        stop=(a == PASSES - 1),
+                    )
+            return bank[:].rearrange("p (t j) -> p j t", t=4)
+
+        def w1_operand(a, b, t):
+            c0 = K * a + 512 * b + P * t
+            return w1_cd[:, 2 * c0 : 2 * (c0 + P)].bitcast(FP4X4), w1_sc[:, c0 : c0 + P]
+
+        w2_q = {}
+        h2_q = []
+
+        def w2_operand(a, b, t):
+            codes, scales = w2_q[a, b]
+            return codes[:, P * t : P * (t + 1)].bitcast(FP8X4), scales[:, P * t : P * (t + 1)]
+
+        def prepare_w2(b):
+            for a in range(PASSES):
+                grouped = held([P, 2048], BF16, "w2_bf%d%d" % (a, b))
+                dealt = grouped[:].rearrange("p (t q i) -> p q i t", t=4, i=4)
+                for h in range(2):
+                    nc.scalar.copy(
+                        dealt[:, 64 * h : 64 * (h + 1), :, :],
+                        w2_raw[a, b, h].rearrange("p i (q t) -> p q i t", t=4),
+                    )
+                w2_q[a, b] = quantise(grouped, 512, "w2_%d%d" % (a, b))
+
+        v_planes = [v_sc[:], v_sc[4:P, :]]
+        prepare_w2(0)
+        h1_q = []
+        for b in range(2):
+            grouped = held([P, 4 * S], BF16, "h1_bf%d" % b)
+            for jq in range(4):
+                sums = first_stage_bank("for_scalar", w1_operand, b, jq, [v_sc[:], v_sc_high[:]])
+                dst = grouped[:, 512 * jq : 512 * (jq + 1)].rearrange("p (j t) -> p j t", t=4)
+                nc.scalar.activation(dst, sums, ACT.Relu)
+            h1_q.append(quantise(grouped, S, "h1_%d" % b))
+
+        prepare_w2(1)
+        for b in range(2):
+            grouped = held([P, 4 * S], BF16, "h2_bf%d" % b)
+            factor = gain_sb[:, 4 * b : 4 * (b + 1)].unsqueeze(1).to_broadcast([P, P, 4])
+            for jq in range(4):
+                sums = first_stage_bank("for_vector", w2_operand, b, jq, v_planes)
+                dst = grouped[:, 512 * jq : 512 * (jq + 1)].rearrange("p (j t) -> p j t", t=4)
+                nc.vector.tensor_tensor(dst, sums, factor, ALU.mult)
+            h2_q.append(quantise(grouped, S, "h2_%d" % b))
+
+        def score_bank(tag, lhs, rhs):
+            bank = psum.tile([P, S], F32, name=tag)
+            for a in range(PASSES):
+                nc.tensor.matmul_mx(
+                    out=bank[:],
+                    lhsT=lhs[a][0].bitcast(FP8X4),
+                    lhsT_scale=lhs[a][1],
+                    rhs=rhs[a][0].bitcast(FP8X4),
+                    rhs_scale=rhs[a][1],
+                    start=(a == 0),
+                    stop=(a == PASSES - 1),
+                )
+            return bank
+
+        def west_operand(m):
+            cols = slice(P * m, P * (m + 1))
+            return [(v2_cd[a][:, cols], v2_sc[4 * a : P, cols]) for a in range(PASSES)]
+
+        e1_sb = []
+        for m in range(8):
+            bank = score_bank("for_scalar", west_operand(m), [(c[:], s[:]) for c, s in h1_q])
+            e1 = held([P, S], F32, "e1_%d" % m)
+            nc.scalar.copy(e1[:], bank[:])
+            e1_sb.append(e1)
+
+        w3_q = {}
+        for u in range(4):
+            for a in range(PASSES):
+                grouped = held([P, 1024], BF16, "w3_bf%d%d" % (a, u))
+                cast = nc.scalar.copy if u == 3 else nc.vector.tensor_copy
+                cast(
+                    grouped[:].rearrange("p (c n i) -> p c i n", n=4, i=4),
+                    w3_raw[a, u].rearrange("p i (c n) -> p c i n", n=4),
+                )
+                w3_q[a, u] = (grouped,)
+            for a in range(PASSES):
+                w3_q[a, u] = quantise(w3_q[a, u][0], HALF, "w3_%d%d" % (a, u))
+
+        for m in range(8):
+            cols = slice(P * (m % 2), P * (m % 2 + 1))
+            lhs = [(w3_q[a, m // 2][0][:, cols], w3_q[a, m // 2][1][:, cols]) for a in range(PASSES)]
+            e3 = score_bank("for_scalar", lhs, [(v_cd[a][:], v_planes[a]) for a in range(PASSES)])
+            size = ring.tile([P, S], F32, name="size")
+            nc.scalar.activation(size[:], e3[:], ACT.Abs)
+            root = ring.tile([P, S], F32, name="root")
+            nc.scalar.activation(root[:], size[:], ACT.Abs_reciprocal_sqrt, bias=1.0)
+            damp = ring.tile([P, S], F32, name="damp")
+            nc.scalar.activation(damp[:], root[:], ACT.Square)
+            e2 = score_bank("for_vector", west_operand(m), [(c[:], s[:]) for c, s in h2_q])
+            best = e1_sb[m]
+            nc.vector.tensor_tensor(best[:], e2[:], e1_sb[m][:], ALU.max)
+            result = ring.tile([P, S], F32, name="result")
+            nc.vector.tensor_tensor(result[:], best[:], damp[:], ALU.mult)
+            nc.sync.dma_start(out[P * m : P * (m + 1), :], result[:])

@@ -30,8 +30,8 @@ def tile_list_bout_contest_scores_kernel(
         ring = ctx.enter_context(tc.tile_pool(name="ring", bufs=3))
         psum = ctx.enter_context(tc.psum_pool(name="psum", bufs=4))
 
-        def held(shape, dtype, name):
-            return keep.tile(shape, dtype, name=name, align_bytes=64)
+        def held(shape, dtype, name, tag=None):
+            return keep.tile(shape, dtype, name=name, tag=tag or name, align_bytes=64)
 
         east = keep.tile([P, S // 16], U16, name="east")
         west = keep.tile([P, S2 // 16], U16, name="west")
@@ -45,7 +45,7 @@ def tile_list_bout_contest_scores_kernel(
         nc.scalar.activation(warm[:, 8:9], warm[:, 0:1], ACT.Abs_reciprocal_sqrt, bias=1.0)
         nc.vector.memset(tab_sc_high[:].bitcast(I32), 0)
 
-        w1_raw = held([P, PASSES * 2 * K], U8, "w1_raw")
+        w1_raw = [held([P, 2 * K], U8, "w1_raw%d" % a) for a in range(PASSES)]
         tab = [held([P, T], I32, "tab%d" % a) for a in range(PASSES)]
         gain_sb = held([P, 8], F32, "gain_sb")
 
@@ -58,10 +58,8 @@ def tile_list_bout_contest_scores_kernel(
         tab_hbm = [tab_words[a].rearrange("p t i -> p (t i)").bitcast(I32) for a in range(PASSES)]
         w2_raw = {}
         nc.sync.dma_start(east[:], offs)
-        nc.sync.dma_start(
-            w1_raw[:].bitcast(I32).rearrange("p (a c) -> p a c", a=PASSES),
-            w1_words.bitcast(I32).rearrange("a p c -> p a c"),
-        )
+        for a in range(PASSES):
+            nc.sync.dma_start(w1_raw[a][:].bitcast(I32), w1_words[a].bitcast(I32))
         for q in range(4):
             nc.sync.dma_start(
                 tab_sc[32 * q : 32 * q + 8, :].bitcast(I32),
@@ -101,14 +99,15 @@ def tile_list_bout_contest_scores_kernel(
 
         w1_cd = held([P, PASSES * 2 * K], U8, "w1_cd")
         w1_sc = held([P, PASSES * K], U8, "w1_sc")
-        nc.vector.tensor_copy(
-            w1_cd[:].bitcast(U16).rearrange("p (g t u q) -> p g u t q", g=4, t=4, q=8),
-            w1_raw[:].bitcast(U16).rearrange("p (g u q t) -> p g u t q", g=4, t=4, q=8),
-        )
+        for a in range(PASSES):
+            nc.vector.tensor_copy(
+                w1_cd[:, 2 * K * a : 2 * K * (a + 1)].bitcast(U16).rearrange("p (g t u q) -> p g u t q", g=2, t=4, q=8),
+                w1_raw[a][:].bitcast(U16).rearrange("p (g u q t) -> p g u t q", g=2, t=4, q=8),
+            )
         v_sc = held([P, S], U8, "v_sc")
         v_sc_high = held([P, S], U8, "v_sc_high")
         v_cd = [held([P, S], U32, "v_cd%d" % a) for a in range(PASSES)]
-        v2_cd = [held([P, S2], U32, "v2_cd%d" % a) for a in range(PASSES)]
+        v2_cd = [held([P, S2], U32, "v2_cd0")]
         v2_sc = held([P, S2], U8, "v2_sc")
         nc.vector.tensor_copy(v_cd[0][:], tab[0][:].bitcast(U32).indirect(east[:]))
         nc.vector.tensor_copy(v_sc[:], tab_sc[:].indirect(east[:]))
@@ -119,8 +118,7 @@ def tile_list_bout_contest_scores_kernel(
         nc.vector.tensor_copy(v_cd[1][:], tab[1][:].bitcast(U32).indirect(east[:]))
         nc.vector.tensor_copy(v_sc_high[:], tab_sc_high[:].indirect(east[:]))
         nc.vector.tensor_copy(v2_sc[:], tab_sc[:].indirect(west[:]))
-        for a in range(PASSES):
-            nc.vector.tensor_copy(v2_cd[a][:], tab[a][:].bitcast(U32).indirect(west[:]))
+        nc.vector.tensor_copy(v2_cd[0][:], tab[0][:].bitcast(U32).indirect(west[:]))
 
         def quantise(grouped, width, name):
             codes = held([P, width], U32, name + "_cd")
@@ -169,9 +167,11 @@ def tile_list_bout_contest_scores_kernel(
 
         v_planes = [v_sc[:], v_sc[4:P, :]]
         prepare_w2(0)
+        v2_cd.append(held([P, S2], U32, "v2_cd1", tag="w2_bf10"))
+        nc.vector.tensor_copy(v2_cd[1][:], tab[1][:].bitcast(U32).indirect(west[:]))
         h1_q = []
         for b in range(2):
-            grouped = held([P, 4 * S], BF16, "h1_bf%d" % b)
+            grouped = held([P, 4 * S], BF16, "h1_bf%d" % b, tag="w2_first%d" % (1 - b))
             for jq in range(4):
                 sums = first_stage_bank("for_scalar", w1_operand, b, jq, [v_sc[:], v_sc_high[:]])
                 dst = grouped[:, 512 * jq : 512 * (jq + 1)].rearrange("p (j t) -> p j t", t=4)
@@ -179,7 +179,20 @@ def tile_list_bout_contest_scores_kernel(
             h1_q.append(quantise(grouped, S, "h1_%d" % b))
 
         prepare_w2(1)
+        w3_q = {}
+
+        def prepare_w3(u):
+            tag = {1: "w2_bf11", 3: "h2_bf1"}.get(u)
+            grouped = held([P, 2048], BF16, "w3_bf%d" % u, tag=tag)
+            for a in range(PASSES):
+                nc.vector.tensor_copy(
+                    grouped[:, 1024 * a : 1024 * (a + 1)].rearrange("p (c n i) -> p c i n", n=4, i=4),
+                    w3_raw[a, u].rearrange("p i (c n) -> p c i n", n=4),
+                )
+            w3_q[u] = quantise(grouped, 512, "w3_%d" % u)
+
         for b in range(2):
+            prepare_w3(b)
             grouped = held([P, 4 * S], BF16, "h2_bf%d" % b)
             factor = gain_sb[:, 4 * b : 4 * (b + 1)].unsqueeze(1).to_broadcast([P, P, 4])
             for jq in range(4):
@@ -213,22 +226,13 @@ def tile_list_bout_contest_scores_kernel(
             nc.scalar.copy(e1[:], bank[:])
             e1_sb.append(e1)
 
-        w3_q = {}
-        for u in range(4):
-            for a in range(PASSES):
-                grouped = held([P, 1024], BF16, "w3_bf%d%d" % (a, u))
-                cast = nc.scalar.copy if u == 3 else nc.vector.tensor_copy
-                cast(
-                    grouped[:].rearrange("p (c n i) -> p c i n", n=4, i=4),
-                    w3_raw[a, u].rearrange("p i (c n) -> p c i n", n=4),
-                )
-                w3_q[a, u] = (grouped,)
-            for a in range(PASSES):
-                w3_q[a, u] = quantise(w3_q[a, u][0], HALF, "w3_%d%d" % (a, u))
+        prepare_w3(2)
+        prepare_w3(3)
 
         for m in range(8):
-            cols = slice(P * (m % 2), P * (m % 2 + 1))
-            lhs = [(w3_q[a, m // 2][0][:, cols], w3_q[a, m // 2][1][:, cols]) for a in range(PASSES)]
+            codes, scales = w3_q[m // 2]
+            cols = [slice(HALF * a + P * (m % 2), HALF * a + P * (m % 2 + 1)) for a in range(PASSES)]
+            lhs = [(codes[:, c], scales[:, c]) for c in cols]
             e3 = score_bank("for_scalar", lhs, [(v_cd[a][:], v_planes[a]) for a in range(PASSES)])
             size = ring.tile([P, S], F32, name="size")
             nc.scalar.activation(size[:], e3[:], ACT.Abs)

from contextlib import ExitStack

import concourse.mybir as mybir

K, T, S, S2 = 1024, 2048, 512, 1024
FLOPS = 5 * 2 * K * K * S

F32 = mybir.dt.float32
BF16 = mybir.dt.bfloat16
I32 = mybir.dt.int32
U32 = mybir.dt.uint32
U16 = mybir.dt.uint16
U8 = mybir.dt.uint8
FP8X4 = mybir.dt.float8_e4m3fn_x4
FP4X4 = mybir.dt.float4_e2m1fn_x4
ACT = mybir.ActivationFunctionType
ALU = mybir.AluOpType

P = 128
PASSES = 2
HALF = 256


def tile_list_bout_contest_scores_kernel(
    tc, tab_words, tab_scales, offs, offs2, w1_words, w1_scales, w2, gain, w3, out
):
    nc = tc.nc
    with ExitStack() as ctx:
        keep = ctx.enter_context(tc.tile_pool(name="keep", bufs=1))
        ring = ctx.enter_context(tc.tile_pool(name="ring", bufs=3))
        psum = ctx.enter_context(tc.psum_pool(name="psum", bufs=4))

        def held(shape, dtype, name, tag=None):
            return keep.tile(shape, dtype, name=name, tag=tag or name, align_bytes=64)

        east = keep.tile([P, S // 16], U16, name="east")
        west = keep.tile([P, S2 // 16], U16, name="west")
        tab_sc = held([P, T], U8, "tab_sc")
        w1_sc_raw = held([P, PASSES * K], U8, "w1_sc_raw")
        tab_sc_high = held([P, T], U8, "tab_sc_high")
        nc.vector.memset(tab_sc[:].bitcast(I32), 0)
        nc.vector.memset(w1_sc_raw[:].bitcast(I32), 0)
        warm = held([P, 16], F32, "warm")
        nc.gpsimd.memset(warm[:, 0:8], 1.0)
        nc.scalar.activation(warm[:, 8:9], warm[:, 0:1], ACT.Abs_reciprocal_sqrt, bias=1.0)
        nc.vector.memset(tab_sc_high[:].bitcast(I32), 0)

        w1_raw = [held([P, 2 * K], U8, "w1_raw%d" % a) for a in range(PASSES)]
        tab = [held([P, T], I32, "tab%d" % a) for a in range(PASSES)]
        gain_sb = held([P, 8], F32, "gain_sb")

        def load_rows(w, a, c0, width, name):
            raw = held([P, 4, width], F32, name)
            rows = w[512 * a : 512 * (a + 1), c0 : c0 + width]
            nc.sync.dma_start(raw[:], rows.rearrange("(p i) c -> p i c", i=4))
            return raw

        tab_hbm = [tab_words[a].rearrange("p t i -> p (t i)").bitcast(I32) for a in range(PASSES)]
        w2_raw = {}
        nc.sync.dma_start(east[:], offs)
        for a in range(PASSES):
            nc.sync.dma_start(w1_raw[a][:].bitcast(I32), w1_words[a].bitcast(I32))
        for q in range(4):
            nc.sync.dma_start(
                tab_sc[32 * q : 32 * q + 8, :].bitcast(I32),
                tab_scales[:, 4 * q : 4 * q + 4, :].bitcast(I32),
            )
        nc.sync.dma_start(tab[0][:], tab_hbm[0])
        for q in range(4):
            nc.sync.dma_start(
                w1_sc_raw[32 * q : 32 * q + 4, :].bitcast(I32).rearrange("r (a c) -> r a c", a=PASSES),
                w1_scales[:, 4 * q : 4 * q + 4, :].bitcast(I32).rearrange("a r c -> r a c"),
            )
        nc.sync.dma_start(tab[1][:], tab_hbm[1])
        for q in range(4):
            nc.sync.dma_start(
                tab_sc_high[32 * q : 32 * q + 4, :].bitcast(I32),
                tab_scales[1, 4 * q : 4 * q + 4, :].bitcast(I32),
            )
        w2_raw[0, 0, 0] = load_rows(w2, 0, 0, HALF, "w2_first0")[:]
        nc.sync.dma_start(west[:], offs2)
        nc.sync.dma_start(
            gain_sb[:].rearrange("p (b t) -> p b t", t=4),
            gain.rearrange("(b p t) -> p b t", p=P, t=4),
        )
        w2_raw[0, 0, 1] = load_rows(w2, 0, HALF, HALF, "w2_first1")[:]
        for b in range(2):
            for a in range(PASSES):
                if (a, b) != (0, 0):
                    raw = load_rows(w2, a, 512 * b, 512, "w2_raw%d%d" % (a, b))
                    for h in range(2):
                        w2_raw[a, b, h] = raw[:, :, HALF * h : HALF * (h + 1)]
        w3_raw = {}
        for b in range(2):
            for a in range(PASSES):
                raw = load_rows(w3, a, 512 * b, 512, "w3_raw%d%d" % (a, b))
                for h in range(2):
                    w3_raw[a, 2 * b + h] = raw[:, :, HALF * h : HALF * (h + 1)]

        w1_cd = held([P, PASSES * 2 * K], U8, "w1_cd")
        w1_sc = held([P, PASSES * K], U8, "w1_sc")
        for a in range(PASSES):
            nc.vector.tensor_copy(
                w1_cd[:, 2 * K * a : 2 * K * (a + 1)].bitcast(U16).rearrange("p (g t u q) -> p g u t q", g=2, t=4, q=8),
                w1_raw[a][:].bitcast(U16).rearrange("p (g u q t) -> p g u t q", g=2, t=4, q=8),
            )
        v_sc = held([P, S], U8, "v_sc")
        v_sc_high = held([P, S], U8, "v_sc_high")
        v_cd = [held([P, S], U32, "v_cd%d" % a) for a in range(PASSES)]
        v2_cd = [held([P, S2], U32, "v2_cd0")]
        v2_sc = held([P, S2], U8, "v2_sc")
        nc.vector.tensor_copy(v_cd[0][:], tab[0][:].bitcast(U32).indirect(east[:]))
        nc.vector.tensor_copy(v_sc[:], tab_sc[:].indirect(east[:]))
        nc.vector.tensor_copy(
            w1_sc[:].rearrange("p (g t u q) -> p g u t q", g=4, t=4, q=16),
            w1_sc_raw[:].rearrange("p (g u q t) -> p g u t q", g=4, t=4, q=16),
        )
        nc.vector.tensor_copy(v_cd[1][:], tab[1][:].bitcast(U32).indirect(east[:]))
        nc.vector.tensor_copy(v_sc_high[:], tab_sc_high[:].indirect(east[:]))
        nc.vector.tensor_copy(v2_sc[:], tab_sc[:].indirect(west[:]))
        nc.vector.tensor_copy(v2_cd[0][:], tab[0][:].bitcast(U32).indirect(west[:]))

        def quantise(grouped, width, name):
            codes = held([P, width], U32, name + "_cd")
            scales = held([P, width], U8, name + "_sc")
            nc.vector.quantize_mx(out=codes[:].bitcast(FP8X4), scales=scales[:], in_=grouped[:])
            return codes, scales

        def first_stage_bank(tag, lhs, b, jq, v_scales):
            bank = psum.tile([P, 4 * P], F32, name=tag)
            cols = slice(P * jq, P * (jq + 1))
            for t in range(4):
                for a in range(PASSES):
                    codes, scales = lhs(a, b, t)
                    nc.tensor.matmul_mx(
                        out=bank[:, P * t : P * (t + 1)],
                        lhsT=codes,
                        lhsT_scale=scales,
                        rhs=v_cd[a][:, cols].bitcast(FP8X4),
                        rhs_scale=v_scales[a][:, cols],
                        start=(a == 0),
                        stop=(a == PASSES - 1),
                    )
            return bank[:].rearrange("p (t j) -> p j t", t=4)

        def w1_operand(a, b, t):
            c0 = K * a + 512 * b + P * t
            return w1_cd[:, 2 * c0 : 2 * (c0 + P)].bitcast(FP4X4), w1_sc[:, c0 : c0 + P]

        w2_q = {}
        h2_q = []

        def w2_operand(a, b, t):
            codes, scales = w2_q[a, b]
            return codes[:, P * t : P * (t + 1)].bitcast(FP8X4), scales[:, P * t : P * (t + 1)]

        def prepare_w2(b):
            for a in range(PASSES):
                grouped = held([P, 2048], BF16, "w2_bf%d%d" % (a, b))
                dealt = grouped[:].rearrange("p (t q i) -> p q i t", t=4, i=4)
                for h in range(2):
                    nc.scalar.copy(
                        dealt[:, 64 * h : 64 * (h + 1), :, :],
                        w2_raw[a, b, h].rearrange("p i (q t) -> p q i t", t=4),
                    )
                w2_q[a, b] = quantise(grouped, 512, "w2_%d%d" % (a, b))

        v_planes = [v_sc[:], v_sc[4:P, :]]
        prepare_w2(0)
        v2_cd.append(held([P, S2], U32, "v2_cd1", tag="w2_bf10"))
        nc.vector.tensor_copy(v2_cd[1][:], tab[1][:].bitcast(U32).indirect(west[:]))
        h1_q = []
        for b in range(2):
            grouped = held([P, 4 * S], BF16, "h1_bf%d" % b, tag="w2_first%d" % (1 - b))
            for jq in range(4):
                sums = first_stage_bank("for_scalar", w1_operand, b, jq, [v_sc[:], v_sc_high[:]])
                dst = grouped[:, 512 * jq : 512 * (jq + 1)].rearrange("p (j t) -> p j t", t=4)
                nc.scalar.activation(dst, sums, ACT.Relu)
            h1_q.append(quantise(grouped, S, "h1_%d" % b))

        prepare_w2(1)
        w3_q = {}

        def prepare_w3(u):
            tag = {1: "w2_bf11", 3: "h2_bf1"}.get(u)
            grouped = held([P, 2048], BF16, "w3_bf%d" % u, tag=tag)
            for a in range(PASSES):
                nc.vector.tensor_copy(
                    grouped[:, 1024 * a : 1024 * (a + 1)].rearrange("p (c n i) -> p c i n", n=4, i=4),
                    w3_raw[a, u].rearrange("p i (c n) -> p c i n", n=4),
                )
            w3_q[u] = quantise(grouped, 512, "w3_%d" % u)

        for b in range(2):
            prepare_w3(b)
            grouped = held([P, 4 * S], BF16, "h2_bf%d" % b)
            factor = gain_sb[:, 4 * b : 4 * (b + 1)].unsqueeze(1).to_broadcast([P, P, 4])
            for jq in range(4):
                sums = first_stage_bank("for_vector", w2_operand, b, jq, v_planes)
                dst = grouped[:, 512 * jq : 512 * (jq + 1)].rearrange("p (j t) -> p j t", t=4)
                nc.vector.tensor_tensor(dst, sums, factor, ALU.mult)
            h2_q.append(quantise(grouped, S, "h2_%d" % b))

        def score_bank(tag, lhs, rhs):
            bank = psum.tile([P, S], F32, name=tag)
            for a in range(PASSES):
                nc.tensor.matmul_mx(
                    out=bank[:],
                    lhsT=lhs[a][0].bitcast(FP8X4),
                    lhsT_scale=lhs[a][1],
                    rhs=rhs[a][0].bitcast(FP8X4),
                    rhs_scale=rhs[a][1],
                    start=(a == 0),
                    stop=(a == PASSES - 1),
                )
            return bank

        def west_operand(m):
            cols = slice(P * m, P * (m + 1))
            return [(v2_cd[a][:, cols], v2_sc[4 * a : P, cols]) for a in range(PASSES)]

        e1_sb = []
        for m in range(8):
            bank = score_bank("for_scalar", west_operand(m), [(c[:], s[:]) for c, s in h1_q])
            e1 = held([P, S], F32, "e1_%d" % m)
            nc.scalar.copy(e1[:], bank[:])
            e1_sb.append(e1)

        prepare_w3(2)
        prepare_w3(3)

        for m in range(8):
            codes, scales = w3_q[m // 2]
            cols = [slice(HALF * a + P * (m % 2), HALF * a + P * (m % 2 + 1)) for a in range(PASSES)]
            lhs = [(codes[:, c], scales[:, c]) for c in cols]
            e3 = score_bank("for_scalar", lhs, [(v_cd[a][:], v_planes[a]) for a in range(PASSES)])
            size = ring.tile([P, S], F32, name="size")
            nc.scalar.activation(size[:], e3[:], ACT.Abs)
            root = ring.tile([P, S], F32, name="root")
            nc.scalar.activation(root[:], size[:], ACT.Abs_reciprocal_sqrt, bias=1.0)
            damp = ring.tile([P, S], F32, name="damp")
            nc.scalar.activation(damp[:], root[:], ACT.Square)
            e2 = score_bank("for_vector", west_operand(m), [(c[:], s[:]) for c, s in h2_q])
            best = e1_sb[m]
            nc.vector.tensor_tensor(best[:], e2[:], e1_sb[m][:], ALU.max)
            result = ring.tile([P, S], F32, name="result")
            nc.vector.tensor_tensor(result[:], best[:], damp[:], ALU.mult)
            nc.sync.dma_start(out[P * m : P * (m + 1), :], result[:])
